import numpy as np, ml_dtypes
CORES = [0,1,2,3]
N = 4
def setup_inputs(rng):
    return {"x": rng.standard_normal((N, 128, 512), dtype=np.float32).astype(ml_dtypes.bfloat16)}
def reference(x):
    g = np.concatenate(list(x), axis=1)
    return {"y": np.broadcast_to(g, (N,) + g.shape)}

from concourse.bass import DstId, RemoteDMATransfer

W = 512

SCRATCH = {
    "land": ("sbuf", [128, 4 * W], "bfloat16"),
}
SEMAPHORES = ["loaded", "arrived", "stored"]


def rank_program(g, core, T, topo):
    rank = T.rank_of(core)
    if rank is None:
        return

    peers = [c for c in T.cores if c != core]
    mine = T.land[:, rank * W:(rank + 1) * W]

    g.sync.dma_start(mine, T.x[:]).then_inc(T.sem.loaded, 16)

    g.wait_ge(T.sem.loaded, 16)
    ids = []
    for p in peers:
        rid, pid, _se = topo.addr(p)
        ids.append(DstId(rid=rid, pnc=pid))
    g.remote_dma_fused(
        [RemoteDMATransfer(dst_ids=ids,
                           dma_engine_mask=topo.mask(core, peers[0]),
                           remote_sem=T.sem.arrived,
                           srcs=[mine],
                           dsts=[mine for _p in peers],
                           alu_op=0)],
        local_sem=T.sem.arrived)

    g.sync.wait_ge(T.sem.loaded, 16)
    g.sync.wait_ge(T.sem.arrived, 16 * (len(peers) + 1))
    g.sync.dma_start(T.y[:], T.land[:]).then_inc(T.sem.stored, 16)
    g.sync.wait_ge(T.sem.stored, 16)
